import numpy as np
import ml_dtypes


def mxq(x, axis, fmt="e4m3"):
    dtype, down = {"e4m3": (ml_dtypes.float8_e4m3fn, 7), "e5m2": (ml_dtypes.float8_e5m2, 14)}[fmt]
    v = np.moveaxis(np.asarray(x, np.float32).astype(ml_dtypes.bfloat16).astype(np.float64), axis, -1)
    blocks = v.reshape(v.shape[:-1] + (-1, 32))
    amax = np.abs(blocks).max(-1, keepdims=True)
    byte = np.maximum(np.where(amax > 0, np.frexp(amax)[1] - 1 + 127, 0) - down, 1)
    scale = np.exp2(byte - 127.0)
    codes = (blocks / scale).astype(np.float32).astype(dtype).astype(np.float64)
    return np.moveaxis((codes * scale).reshape(v.shape), -1, axis)


WIDE = False


def mx_kscale(k):
    if not WIDE:
        return np.ones(k)
    levels = np.array([10, -10, 5, -5, 0])
    if k % 512:
        return np.exp2(np.random.permutation(np.resize(levels, k // 32))).repeat(32)
    a = np.empty((k // 512, 16))
    for p in range(k // 512):
        a[p, :8] = np.random.permutation(np.resize(levels, 8))
        for g in range(8):
            far = levels[np.abs(levels - a[p, g]) >= 10]
            a[p, g + 8] = far[np.random.randint(len(far))]
    return np.exp2(a.ravel()).repeat(32)


def f64(x):
    return np.asarray(x).astype(np.float64)


def striped(idx):
    return np.tile(idx.reshape(-1, 16).T, (8, 1)).astype(np.uint16)


def unstriped(offs):
    return offs[:16].T.reshape(-1).astype(np.int64)


def striped8(idx):
    return np.concatenate([x.reshape(-1, 16).T for x in idx]).astype(np.uint16)


def runs(offs, k):
    lists = np.stack([offs[16 * r : 16 * r + 16].T.reshape(-1) for r in range(8)]).astype(np.int64)
    return lists[np.arange(k) % 512 // 64]


def pack_weight(w):
    k, n = w.shape
    w = f64(np.asarray(w, np.float32).astype(ml_dtypes.bfloat16)).reshape(k // 32, 32, n)
    amax = np.abs(w).max(1)
    byte = np.clip(np.where(amax > 0, np.frexp(amax)[1] - 1 + 127 - 7, 1), 1, 254)
    scaled = (w * np.exp2(127.0 - byte)[:, None, :]).reshape(k, n).astype(np.float32)
    words = np.ascontiguousarray(scaled.reshape(k // 512, 128, 4, n).transpose(0, 1, 3, 2)).astype(ml_dtypes.float8_e4m3fn).view(np.uint8)
    return words, np.ascontiguousarray(byte.astype(np.uint8).reshape(k // 512, 16, n))


def unpack_weight(words, scales):
    g, p, n, _ = words.shape
    vals = np.ascontiguousarray(words).view(ml_dtypes.float8_e4m3fn).astype(np.float64) * np.repeat(np.exp2(scales.astype(np.float64) - 127.0), 8, axis=1)[..., None]
    return vals.transpose(0, 1, 3, 2).reshape(g * 512, n)


def sigmoid(v):
    return 1.0 / (1.0 + np.exp(-np.maximum(v, -700.0)))

def planes(y):
    n, m = y.shape
    v = y.astype(np.float32).astype(ml_dtypes.bfloat16).astype(np.float64).reshape(n // 32, 32, m)
    top = np.abs(v).max(1)
    byte = np.clip(np.where(top > 0, np.frexp(top)[1] - 1 + 127 - 7, 1), 1, 254)
    codes = (v * np.exp2(127.0 - byte)[:, None, :]).reshape(n, m).astype(np.float32).astype(ml_dtypes.float8_e4m3fn).view(np.uint8)
    words = codes.reshape(n // 512, 128, 4, m).transpose(0, 1, 3, 2)
    return np.ascontiguousarray(words), np.ascontiguousarray(byte.astype(np.uint8).reshape(n // 512, 16, m))


K, T, S, N, H = 512, 2048, 512, 512, 512


def setup_inputs():
    n = np.random.standard_normal
    s = mx_kscale(K)[:, None]
    u = mx_kscale(H)
    packed_xT = pack_weight(n((K, T)) * s)
    packed_w1 = pack_weight(n((K, H)) / np.sqrt(K) / s)
    packed_w2 = pack_weight(n((K, H)) / np.sqrt(K) / s)
    packed_w3 = pack_weight(n((H, N)) / np.sqrt(H) / u[:, None])
    return {
        "x_words": packed_xT[0],
        "x_scales": packed_xT[1],
        "w1_words": packed_w1[0],
        "w1_scales": packed_w1[1],
        "w2_words": packed_w2[0],
        "w2_scales": packed_w2[1],
        "gn": (np.random.uniform(0.5, 1.5, (H, 1)) * u[:, None]).astype(np.float32),
        "w3_words": packed_w3[0],
        "w3_scales": packed_w3[1],
        "res": (2 * n((N, S))).astype(np.float32),
        "offs": striped(np.random.permutation(T)[:S]),
        "two": striped(np.random.permutation(T)[:S]),
        "nb": striped8(np.stack([np.random.permutation(S) for _ in range(8)])),
    }


def reference(x_words, x_scales, w1_words, w1_scales, w2_words, w2_scales, gn, w3_words, w3_scales, res, offs, two, nb):
    x_two = unpack_weight(x_words, x_scales)[:, unstriped(two)]
    c = sigmoid(unpack_weight(w2_words, w2_scales).T @ x_two)
    cn = c[np.arange(H)[:, None], runs(nb, H)]
    xq = unpack_weight(x_words, x_scales)[:, unstriped(offs)]
    y = unpack_weight(w1_words, w1_scales).T @ xq
    z = f64(gn) * (((4.0 * (c * cn)) / (c + cn)) * (y[np.arange(H)[:, None], runs(nb, H)] - y))
    out_0 = f64(res) + (unpack_weight(w3_words, w3_scales).T @ mxq(z, 0, "e4m3"))
    return (out_0,) + planes(out_0)

@@ -1,0 +1,249 @@
+from contextlib import ExitStack
+
+import concourse.mybir as mybir
+
+F32 = mybir.dt.float32
+BF16 = mybir.dt.bfloat16
+I32 = mybir.dt.int32
+U32 = mybir.dt.uint32
+U16 = mybir.dt.uint16
+U8 = mybir.dt.uint8
+FP8X4 = mybir.dt.float8_e4m3fn_x4
+ACT = mybir.ActivationFunctionType
+ALU = mybir.AluOpType
+
+P = 128
+T = 2048
+S = 512
+HALF = 256
+FLOPS = 3 * 2 * 512 * 512 * 512
+
+
+def words_of(packed):
+    return packed[0].rearrange("p n t -> p (n t)").bitcast(I32)
+
+
+def tile_picked_harmflux_none_po_kernel(
+    tc, x_words, x_scales, w1_words, w1_scales, w2_words, w2_scales, gn, w3_words, w3_scales, res, offs, two, nb,
+    out_0, out_1, out_2,
+):
+    nc = tc.nc
+    with ExitStack() as ctx:
+        lists = ctx.enter_context(tc.tile_pool(name="lists", bufs=1))
+        keep = ctx.enter_context(tc.tile_pool(name="keep", bufs=1))
+        psum = ctx.enter_context(tc.psum_pool(name="psum", bufs=8))
+
+        def sb(name, shape, dtype, tag=None):
+            return keep.tile(shape, dtype, name=name, tag=tag or name, align_bytes=64)
+
+        def bank(name):
+            return psum.tile([P, 512], F32, name=name, tag="bank")
+
+        def load_scale_rows(queue, plane, first, scales):
+            for q in range(4):
+                queue.dma_start(
+                    out=plane[32 * q + first : 32 * q + first + 4, :].bitcast(I32),
+                    in_=scales[0, 4 * q : 4 * q + 4, :].bitcast(I32),
+                )
+
+        two_sb = lists.tile([P, S // 16], U16, name="two_sb")
+        offs_sb = lists.tile([P, S // 16], U16, name="offs_sb")
+        nb_sb = lists.tile([P, S // 16], U16, name="nb_sb")
+
+        zeros = sb("zeros", [P, P], F32, "wide")
+        ident = sb("ident", [P, P], F32)
+        xs = sb("xs", [P, T], U8)
+        ws2 = sb("ws2", [P, 512], U8, "ws_a")
+        ws1 = sb("ws1", [P, 512], U8)
+        w2 = sb("w2", [P, 512], I32, "w_a")
+        w1 = sb("w1", [P, 512], I32)
+        gain = sb("gain", [P, 4], F32)
+        warm = sb("warm", [P, 2], F32)
+
+        nc.gpsimd.memset(zeros[:], 0.0)
+        nc.gpsimd.memset(xs[:].bitcast(I32), 0)
+        nc.gpsimd.affine_select(
+            out=ident[:], in_=zeros[:], compare_op=ALU.not_equal, fill=1.0, base=0, pattern=[[-1, P]], channel_multiplier=1
+        )
+        nc.vector.memset(ws2[:].bitcast(I32), 0)
+        nc.vector.memset(ws1[:].bitcast(I32), 0)
+        nc.vector.memset(warm[:], 0.0)
+        nc.scalar.activation(out=warm[:, 1:2], in_=warm[:, 0:1], func=ACT.Exp)
+
+        nc.sync.dma_start(two_sb[:], two)
+        nc.sync.dma_start(offs_sb[:], offs)
+        nc.sync.dma_start(nb_sb[:], nb)
+        load_scale_rows(nc.sync, xs, 0, x_scales)
+        xw = sb("xw", [P, T], I32, "wide")
+        nc.sync.dma_start(out=xw[:], in_=words_of(x_words))
+        nc.gpsimd.dma_start(out=w2[:], in_=words_of(w2_words))
+        nc.gpsimd.dma_start(out=w1[:], in_=words_of(w1_words))
+        nc.gpsimd.dma_start(out=gain[:], in_=gn.rearrange("(p t) o -> p (t o)", t=4))
+        load_scale_rows(nc.scalar, ws2, 0, w2_scales)
+        load_scale_rows(nc.scalar, ws1, 0, w1_scales)
+
+        def deal_aside(name, src, dtype):
+            dealt = sb(name, [P, 512], dtype)
+            nc.gpsimd.tensor_copy(
+                out=dealt[:].rearrange("p (t m) -> p t m", t=4), in_=src[:].rearrange("p (m t) -> p t m", t=4)
+            )
+            return dealt
+
+        def pick_scales(name, picks):
+            picked = sb(name, [P, S], U8)
+            nc.vector.tensor_copy(picked[:], xs[:].indirect(picks[:]))
+            return picked
+
+        def pick_words(name, picks):
+            picked = sb(name, [P, S], U32)
+            nc.vector.tensor_copy(picked[:], xw[:].bitcast(U32).indirect(picks[:]))
+            return picked
+
+        def product(out, weights, plane, first, t, codes, scales):
+            cols = slice(P * t, P * (t + 1))
+            nc.tensor.matmul_mx(
+                out=out, lhsT=weights[:, cols].bitcast(FP8X4), lhsT_scale=plane[first:P, cols],
+                rhs=codes.bitcast(FP8X4), rhs_scale=scales, start=True, stop=True,
+            )
+
+        two_scales = pick_scales("two_scales", two_sb)
+        offs_scales = pick_scales("offs_scales", offs_sb)
+        two_words = pick_words("two_words", two_sb)
+        w2d = deal_aside("w2d", w2, I32)
+        ws2d = deal_aside("ws2d", ws2, U8)
+        expo = []
+        for t in range(4):
+            acc = bank("a%d" % t)
+            product(acc[:], w2d, ws2d, 0, t, two_words[:], two_scales[:])
+            e_t = sb("expo%d" % t, [P, S], F32)
+            nc.scalar.activation(out=e_t[:], in_=acc[:], func=ACT.Exp, scale=-1.0)
+            expo.append(e_t)
+
+        offs_words = pick_words("offs_words", offs_sb)
+        w1d = deal_aside("w1d", w1, I32)
+        ws1d = deal_aside("ws1d", ws1, U8)
+        w3 = sb("w3", [P, 512], I32, "w_a")
+        ws3 = sb("ws3", [P, 512], U8, "ws_a")
+        res_sb = sb("res_sb", [P, 4, S], F32, "wide")
+        nc.gpsimd.memset(ws3[:].bitcast(I32), 0)
+        nc.sync.dma_start(out=w3[:], in_=words_of(w3_words))
+        load_scale_rows(nc.sync, ws3, 0, w3_scales)
+        nc.sync.dma_start(out=res_sb[:], in_=res.rearrange("(p t) j -> p t j", t=4))
+        vals = []
+        for t in range(4):
+            acc = bank("y%d" % t)
+            product(acc[:], w1d, ws1d, 0, t, offs_words[:], offs_scales[:])
+            y_t = sb("vals%d" % t, [P, S], F32)
+            nc.scalar.activation(out=y_t[:], in_=acc[:], func=ACT.Copy, scale=gain[:, t : t + 1])
+            vals.append(y_t)
+
+        def turned_sum(name, h, u, own, fetched):
+            acc = bank(name)
+            parts = [(src, first) for src, first in ((own, HALF * h), (fetched, 0))]
+            steps = [(src[2 * u + e], first, e, b) for src, first in parts for e in range(2) for b in range(2)]
+            for n, (src, first, e, b) in enumerate(steps):
+                nc.tensor.matmul(
+                    acc[:, HALF * e + P * b : HALF * e + P * (b + 1)],
+                    lhsT=src[:, first + P * b : first + P * (b + 1)], rhs=ident[:],
+                    start=(n == 0), stop=(n == len(steps) - 1), is_transpose=True,
+                )
+            return acc
+
+        def pairs(ap):
+            return ap.rearrange("p (e j) -> p j e", e=2)
+
+        def woven(ap):
+            return ap.rearrange("p (j e) -> p j e", e=2)
+
+        def nb_slice(h):
+            return nb_sb[:, 16 * h : 16 * (h + 1)]
+
+        def conductance(h):
+            fetched = []
+            for t in range(4):
+                g = sb("en%d_%d" % (h, t), [P, HALF], F32)
+                nc.vector.tensor_copy(g[:], expo[t][:].indirect(nb_slice(h)))
+                fetched.append(g)
+            factors = []
+            for u in range(2):
+                acc = turned_sum("s%d_%d" % (h, u), h, u, expo, fetched)
+                root = sb("root%d_%d" % (h, u), [P, 512], F32)
+                nc.scalar.activation(out=woven(root[:]), in_=pairs(acc[:]), func=ACT.Abs_reciprocal_sqrt, scale=0.5, bias=1.0)
+                factor = sb("factor%d_%d" % (h, u), [P, 512], F32)
+                nc.scalar.activation(out=factor[:], in_=root[:], func=ACT.Square)
+                factors.append(factor)
+            return factors
+
+        def difference(h):
+            fetched = []
+            for t in range(4):
+                g = sb("yn%d_%d" % (h, t), [P, HALF], F32)
+                nc.vector.tensor_scalar(g[:], vals[t][:].indirect(nb_slice(h)), -1.0, 0.0, ALU.mult, ALU.add)
+                fetched.append(g)
+            return [turned_sum("d%d_%d" % (h, u), h, u, vals, fetched) for u in range(2)]
+
+        def flux(h, factors, diffs):
+            back = bank("z%d" % h)
+            for u in range(2):
+                zt = sb("zt%d_%d" % (h, u), [P, 512], BF16)
+                nc.vector.scalar_tensor_tensor(woven(zt[:]), pairs(diffs[u][:]), -2.0, woven(factors[u][:]), ALU.mult, ALU.mult)
+                for b in range(2):
+                    nc.tensor.transpose(
+                        back[:, HALF * u + P * b : HALF * u + P * (b + 1)],
+                        zt[:].bitcast(F32)[:, P * b : P * (b + 1)], ident[:],
+                    )
+            z = sb("z%d" % h, [P, 4 * HALF], BF16)
+            nc.scalar.copy(out=woven(z[:].bitcast(F32)), in_=pairs(back[:]))
+            return z
+
+        def quantise(codes, scales, values):
+            nc.vector.quantize_mx(out=codes.bitcast(FP8X4), scales=scales, in_=values)
+
+        out_rows = out_0.rearrange("(p t) j -> p t j", t=4)
+        out_codes = sb("out_codes", [P, S], U32)
+        out_scales = sb("out_scales", [P, S], U8)
+
+        def last_layer(h, z, w3d, ws3d):
+            cols = slice(HALF * h, HALF * (h + 1))
+            z_codes = sb("z_codes%d" % h, [P, HALF], U32)
+            z_scales = sb("z_scales%d" % h, [P, HALF], U8)
+            quantise(z_codes[:], z_scales[:], z[:])
+            result = sb("result%d" % h, [P, 4, HALF], F32)
+            for v in range(2):
+                acc = bank("o%d_%d" % (h, v))
+                for e in range(2):
+                    product(acc[:, HALF * e : HALF * (e + 1)], w3d, ws3d, 0, 2 * v + e, z_codes[:], z_scales[:])
+                nc.vector.tensor_tensor(
+                    result[:, 2 * v : 2 * v + 2, :], acc[:].rearrange("p (e j) -> p e j", e=2),
+                    res_sb[:, 2 * v : 2 * v + 2, cols], ALU.add,
+                )
+            nc.sync.dma_start(out=out_rows[:, :, cols], in_=result[:])
+            rounded = sb("rounded%d" % h, [P, 4 * HALF], BF16)
+            nc.scalar.copy(
+                out=rounded[:].rearrange("p (c i t) -> p c t i", i=4, t=4),
+                in_=result[:].rearrange("p t (c i) -> p c t i", i=4),
+            )
+            return rounded
+
+        def hand_on(h, rounded):
+            cols = slice(HALF * h, HALF * (h + 1))
+            quantise(out_codes[:, cols], out_scales[:, cols], rounded[:])
+            nc.sync.dma_start(out=words_of(out_1)[:, cols], in_=out_codes[:, cols].bitcast(I32))
+
+        factors0 = conductance(0)
+        diffs0 = difference(0)
+        factors1 = conductance(1)
+        z0 = flux(0, factors0, diffs0)
+        w3d = deal_aside("w3d", w3, I32)
+        ws3d = deal_aside("ws3d", ws3, U8)
+        diffs1 = difference(1)
+        rounded0 = last_layer(0, z0, w3d, ws3d)
+        z1 = flux(1, factors1, diffs1)
+        rounded1 = last_layer(1, z1, w3d, ws3d)
+        hand_on(0, rounded0)
+        hand_on(1, rounded1)
+        for q in range(4):
+            queue = nc.sync if q % 2 else nc.scalar
+            queue.dma_start(
+                out=out_2[0, 4 * q : 4 * q + 4, :].bitcast(I32), in_=out_scales[32 * q : 32 * q + 4, :].bitcast(I32)
+            )

@@ -31,18 +31,22 @@ def tile_picked_harmflux_none_po_kernel(
     with ExitStack() as ctx:
         lists = ctx.enter_context(tc.tile_pool(name="lists", bufs=1))
         keep = ctx.enter_context(tc.tile_pool(name="keep", bufs=1))
-        psum = ctx.enter_context(tc.psum_pool(name="psum", bufs=8))
+        stage = ctx.enter_context(tc.tile_pool(name="stage", bufs=1))
+        psum = ctx.enter_context(tc.psum_pool(name="psum", bufs=1))
 
-        def sb(name, shape, dtype, tag=None):
-            return keep.tile(shape, dtype, name=name, tag=tag or name, align_bytes=64)
+        def sb(name, shape, dtype):
+            return keep.tile(shape, dtype, name=name, align_bytes=64)
 
-        def bank(name):
-            return psum.tile([P, 512], F32, name=name, tag="bank")
+        def staged(name, shape, dtype, offset):
+            return stage.tile(shape, dtype, name=name, offset=offset, align_bytes=64)
 
-        def load_scale_rows(queue, plane, first, scales):
+        def bank(name, number):
+            return psum.tile([P, 512], F32, name=name, tag="bank%d" % number)
+
+        def load_scale_rows(plane, scales):
             for q in range(4):
-                queue.dma_start(
-                    out=plane[32 * q + first : 32 * q + first + 4, :].bitcast(I32),
+                nc.sync.dma_start(
+                    out=plane[32 * q : 32 * q + 4, :].bitcast(I32),
                     in_=scales[0, 4 * q : 4 * q + 4, :].bitcast(I32),
                 )
 
@@ -50,42 +54,56 @@ def tile_picked_harmflux_none_po_kernel(
         offs_sb = lists.tile([P, S // 16], U16, name="offs_sb")
         nb_sb = lists.tile([P, S // 16], U16, name="nb_sb")
 
-        zeros = sb("zeros", [P, P], F32, "wide")
+        zeros = staged("zeros", [P, 27648 // 4], F32, 0)
         ident = sb("ident", [P, P], F32)
         xs = sb("xs", [P, T], U8)
-        ws2 = sb("ws2", [P, 512], U8, "ws_a")
-        ws1 = sb("ws1", [P, 512], U8)
-        w2 = sb("w2", [P, 512], I32, "w_a")
-        w1 = sb("w1", [P, 512], I32)
-        gain = sb("gain", [P, 4], F32)
-        warm = sb("warm", [P, 2], F32)
 
-        nc.gpsimd.memset(zeros[:], 0.0)
         nc.gpsimd.memset(xs[:].bitcast(I32), 0)
+        nc.gpsimd.memset(zeros[:, :P], 0.0)
         nc.gpsimd.affine_select(
-            out=ident[:], in_=zeros[:], compare_op=ALU.not_equal, fill=1.0, base=0, pattern=[[-1, P]], channel_multiplier=1
+            out=ident[:], in_=zeros[:, :P], compare_op=ALU.not_equal, fill=1.0, base=0, pattern=[[-1, P]], channel_multiplier=1
         )
-        nc.vector.memset(ws2[:].bitcast(I32), 0)
-        nc.vector.memset(ws1[:].bitcast(I32), 0)
-        nc.vector.memset(warm[:], 0.0)
-        nc.scalar.activation(out=warm[:, 1:2], in_=warm[:, 0:1], func=ACT.Exp)
-
         nc.sync.dma_start(two_sb[:], two)
         nc.sync.dma_start(offs_sb[:], offs)
         nc.sync.dma_start(nb_sb[:], nb)
-        load_scale_rows(nc.sync, xs, 0, x_scales)
-        xw = sb("xw", [P, T], I32, "wide")
-        nc.sync.dma_start(out=xw[:], in_=words_of(x_words))
-        nc.gpsimd.dma_start(out=w2[:], in_=words_of(w2_words))
-        nc.gpsimd.dma_start(out=w1[:], in_=words_of(w1_words))
-        nc.gpsimd.dma_start(out=gain[:], in_=gn.rearrange("(p t) o -> p (t o)", t=4))
-        load_scale_rows(nc.scalar, ws2, 0, w2_scales)
-        load_scale_rows(nc.scalar, ws1, 0, w1_scales)
+        load_scale_rows(xs, x_scales)
 
-        def deal_aside(name, src, dtype):
+        w2 = staged("w2", [P, 512], I32, 2048)
+        ws2 = staged("ws2", [P, 512], U8, 4096)
+        xw = staged("xw", [P, T], I32, 6144)
+        w1 = staged("w1", [P, 512], I32, 14336)
+        ws1 = staged("ws1", [P, 512], U8, 16384)
+        w3 = staged("w3", [P, 512], I32, 24576)
+        ws3 = staged("ws3", [P, 512], U8, 26624)
+        gain_rows = staged("gain_rows", [P, P], F32, 27136)
+        gain = staged("gain", [P, 4], F32, 0)
+        nc.gpsimd.memset(ws2[:].bitcast(I32), 0)
+        nc.gpsimd.memset(gain_rows[:], 0.0)
+        nc.gpsimd.memset(ws1[:].bitcast(I32), 0)
+        nc.gpsimd.memset(ws3[:].bitcast(I32), 0)
+        nc.sync.dma_start(out=xw[:], in_=words_of(x_words))
+        nc.sync.dma_start(out=w2[:], in_=words_of(w2_words))
+        load_scale_rows(ws2, w2_scales)
+        nc.sync.dma_start(out=w1[:], in_=words_of(w1_words))
+        nc.sync.dma_start(
+            out=gain_rows[0:4, :].rearrange("t (g i) -> t g i", g=8), in_=gn.rearrange("(g t i) o -> t g (i o)", g=8, t=4)
+        )
+        load_scale_rows(ws1, w1_scales)
+        nc.sync.dma_start(out=w3[:], in_=words_of(w3_words))
+        load_scale_rows(ws3, w3_scales)
+
+        def deal(name, src, dtype):
             dealt = sb(name, [P, 512], dtype)
-            nc.gpsimd.tensor_copy(
-                out=dealt[:].rearrange("p (t m) -> p t m", t=4), in_=src[:].rearrange("p (m t) -> p t m", t=4)
+            nc.vector.tensor_copy(
+                out=dealt[:].rearrange("p (t m) -> p m t", t=4), in_=src[:].rearrange("p (m t) -> p m t", t=4)
+            )
+            return dealt
+
+        def deal_runs(name, src, dtype):
+            dealt = sb(name, [P, 512], dtype)
+            nc.vector.tensor_copy(
+                out=dealt[:].bitcast(I32).rearrange("p (t g i) -> p t g i", t=4, g=8),
+                in_=src[:].bitcast(I32).rearrange("p (g t i) -> p t g i", t=4, g=8),
             )
             return dealt
 
@@ -94,82 +112,80 @@ def tile_picked_harmflux_none_po_kernel(
             nc.vector.tensor_copy(picked[:], xs[:].indirect(picks[:]))
             return picked
 
-        def pick_words(name, picks):
-            picked = sb(name, [P, S], U32)
+        def pick_words(picked, picks):
             nc.vector.tensor_copy(picked[:], xw[:].bitcast(U32).indirect(picks[:]))
             return picked
 
-        def product(out, weights, plane, first, t, codes, scales):
+        def product(out, weights, plane, t, codes, scales):
             cols = slice(P * t, P * (t + 1))
             nc.tensor.matmul_mx(
-                out=out, lhsT=weights[:, cols].bitcast(FP8X4), lhsT_scale=plane[first:P, cols],
+                out=out, lhsT=weights[:, cols].bitcast(FP8X4), lhsT_scale=plane[:, cols],
                 rhs=codes.bitcast(FP8X4), rhs_scale=scales, start=True, stop=True,
             )
 
         two_scales = pick_scales("two_scales", two_sb)
         offs_scales = pick_scales("offs_scales", offs_sb)
-        two_words = pick_words("two_words", two_sb)
-        w2d = deal_aside("w2d", w2, I32)
-        ws2d = deal_aside("ws2d", ws2, U8)
+        two_words = pick_words(sb("two_words", [P, S], U32), two_sb)
+        w2d = deal_runs("w2d", w2, I32)
+        ws2d = deal_runs("ws2d", ws2, U8)
         expo = []
         for t in range(4):
-            acc = bank("a%d" % t)
-            product(acc[:], w2d, ws2d, 0, t, two_words[:], two_scales[:])
+            acc = bank("a%d" % t, t)
+            product(acc[:], w2d, ws2d, t, two_words[:], two_scales[:])
             e_t = sb("expo%d" % t, [P, S], F32)
             nc.scalar.activation(out=e_t[:], in_=acc[:], func=ACT.Exp, scale=-1.0)
             expo.append(e_t)
 
-        offs_words = pick_words("offs_words", offs_sb)
-        w1d = deal_aside("w1d", w1, I32)
-        ws1d = deal_aside("ws1d", ws1, U8)
-        w3 = sb("w3", [P, 512], I32, "w_a")
-        ws3 = sb("ws3", [P, 512], U8, "ws_a")
-        res_sb = sb("res_sb", [P, 4, S], F32, "wide")
-        nc.gpsimd.memset(ws3[:].bitcast(I32), 0)
-        nc.sync.dma_start(out=w3[:], in_=words_of(w3_words))
-        load_scale_rows(nc.sync, ws3, 0, w3_scales)
+        offs_words = pick_words(staged("offs_words", [P, S], U32, 4032), offs_sb)
+        w1d = deal_runs("w1d", w1, I32)
+        ws1d = deal_runs("ws1d", ws1, U8)
+        gain_turned = bank("gain_turned", 7)
+        nc.tensor.transpose(gain_turned[:, :P], gain_rows[:], ident[:])
+        nc.scalar.activation(out=gain[:], in_=gain_turned[:, 0:4], func=ACT.Copy, scale=-2.0)
+        res_sb = staged("res_sb", [P, 4, S], F32, 6144)
         nc.sync.dma_start(out=res_sb[:], in_=res.rearrange("(p t) j -> p t j", t=4))
         vals = []
         for t in range(4):
-            acc = bank("y%d" % t)
-            product(acc[:], w1d, ws1d, 0, t, offs_words[:], offs_scales[:])
+            acc = bank("y%d" % t, 4 + t)
+            product(acc[:], w1d, ws1d, t, offs_words[:], offs_scales[:])
             y_t = sb("vals%d" % t, [P, S], F32)
             nc.scalar.activation(out=y_t[:], in_=acc[:], func=ACT.Copy, scale=gain[:, t : t + 1])
             vals.append(y_t)
 
-        def turned_sum(name, h, u, own, fetched):
-            acc = bank(name)
-            parts = [(src, first) for src, first in ((own, HALF * h), (fetched, 0))]
-            steps = [(src[2 * u + e], first, e, b) for src, first in parts for e in range(2) for b in range(2)]
-            for n, (src, first, e, b) in enumerate(steps):
+        def turned_sum(name, number, b, own, fetched):
+            acc = bank(name, number)
+            steps = [(own[t][:, P * b : P * (b + 1)], t) for t in range(4)]
+            steps = steps + [(fetched[t][:, P * (b % 2) : P * (b % 2 + 1)], t) for t in range(4)]
+            for n, (src, t) in enumerate(steps):
                 nc.tensor.matmul(
-                    acc[:, HALF * e + P * b : HALF * e + P * (b + 1)],
-                    lhsT=src[:, first + P * b : first + P * (b + 1)], rhs=ident[:],
+                    acc[:, P * t : P * (t + 1)], lhsT=src, rhs=ident[:],
                     start=(n == 0), stop=(n == len(steps) - 1), is_transpose=True,
                 )
             return acc
 
-        def pairs(ap):
-            return ap.rearrange("p (e j) -> p j e", e=2)
+        def paired(ap):
+            return ap.rearrange("j (t g i) -> j g t i", t=4, g=8)
 
         def woven(ap):
-            return ap.rearrange("p (j e) -> p j e", e=2)
+            return ap.rearrange("j (g t i) -> j g t i", t=4, g=8)
 
         def nb_slice(h):
             return nb_sb[:, 16 * h : 16 * (h + 1)]
 
+        expo_near = staged("expo_near", [P, 4 * S], F32, 16320)
+
         def conductance(h):
             fetched = []
             for t in range(4):
-                g = sb("en%d_%d" % (h, t), [P, HALF], F32)
-                nc.vector.tensor_copy(g[:], expo[t][:].indirect(nb_slice(h)))
+                g = expo_near[:, S * t + HALF * h : S * t + HALF * (h + 1)]
+                nc.vector.tensor_copy(g, expo[t][:].indirect(nb_slice(h)))
                 fetched.append(g)
             factors = []
-            for u in range(2):
-                acc = turned_sum("s%d_%d" % (h, u), h, u, expo, fetched)
-                root = sb("root%d_%d" % (h, u), [P, 512], F32)
-                nc.scalar.activation(out=woven(root[:]), in_=pairs(acc[:]), func=ACT.Abs_reciprocal_sqrt, scale=0.5, bias=1.0)
-                factor = sb("factor%d_%d" % (h, u), [P, 512], F32)
+            for b in (2 * h, 2 * h + 1):
+                acc = turned_sum("s%d" % b, b, b, expo, fetched)
+                root = staged("root0", [P, 512], F32, 0) if b == 0 else sb("root%d" % b, [P, 512], F32)
+                nc.scalar.activation(out=woven(root[:]), in_=paired(acc[:]), func=ACT.Abs_reciprocal_sqrt, scale=0.5, bias=1.0)
+                factor = sb("factor%d" % b, [P, 512], F32)
                 nc.scalar.activation(out=factor[:], in_=root[:], func=ACT.Square)
                 factors.append(factor)
             return factors
@@ -180,21 +196,7 @@ def tile_picked_harmflux_none_po_kernel(
                 g = sb("yn%d_%d" % (h, t), [P, HALF], F32)
                 nc.vector.tensor_scalar(g[:], vals[t][:].indirect(nb_slice(h)), -1.0, 0.0, ALU.mult, ALU.add)
                 fetched.append(g)
-            return [turned_sum("d%d_%d" % (h, u), h, u, vals, fetched) for u in range(2)]
-
-        def flux(h, factors, diffs):
-            back = bank("z%d" % h)
-            for u in range(2):
-                zt = sb("zt%d_%d" % (h, u), [P, 512], BF16)
-                nc.vector.scalar_tensor_tensor(woven(zt[:]), pairs(diffs[u][:]), -2.0, woven(factors[u][:]), ALU.mult, ALU.mult)
-                for b in range(2):
-                    nc.tensor.transpose(
-                        back[:, HALF * u + P * b : HALF * u + P * (b + 1)],
-                        zt[:].bitcast(F32)[:, P * b : P * (b + 1)], ident[:],
-                    )
-            z = sb("z%d" % h, [P, 4 * HALF], BF16)
-            nc.scalar.copy(out=woven(z[:].bitcast(F32)), in_=pairs(back[:]))
-            return z
+            return [turned_sum("d%d" % b, 4 + b, b, vals, fetched) for b in (2 * h, 2 * h + 1)]
 
         def quantise(codes, scales, values):
             nc.vector.quantize_mx(out=codes.bitcast(FP8X4), scales=scales, in_=values)
@@ -203,45 +205,47 @@ def tile_picked_harmflux_none_po_kernel(
         out_codes = sb("out_codes", [P, S], U32)
         out_scales = sb("out_scales", [P, S], U8)
 
-        def last_layer(h, z, w3d, ws3d):
-            cols = slice(HALF * h, HALF * (h + 1))
-            z_codes = sb("z_codes%d" % h, [P, HALF], U32)
-            z_scales = sb("z_scales%d" % h, [P, HALF], U8)
+        def flux(b, factor, diff):
+            zt = sb("zt%d" % b, [P, 512], BF16)
+            nc.vector.tensor_tensor(woven(zt[:]), paired(diff[:]), woven(factor[:]), ALU.mult)
+            back = bank("z%d" % b, b)
+            for u in range(2):
+                nc.tensor.transpose(back[:, P * u : P * (u + 1)], zt[:].bitcast(F32)[:, u : 2 * P : 2], ident[:])
+            z = sb("z%d" % b, [P, 512], BF16)
+            nc.scalar.copy(
+                out=z[:].bitcast(F32).rearrange("p (j u) -> p j u", u=2),
+                in_=back[:, : 2 * P].rearrange("p (u j) -> p j u", u=2),
+            )
+            z_codes = sb("z_codes%d" % b, [P, P], U32)
+            z_scales = sb("z_scales%d" % b, [P, P], U8)
             quantise(z_codes[:], z_scales[:], z[:])
-            result = sb("result%d" % h, [P, 4, HALF], F32)
-            for v in range(2):
-                acc = bank("o%d_%d" % (h, v))
-                for e in range(2):
-                    product(acc[:, HALF * e : HALF * (e + 1)], w3d, ws3d, 0, 2 * v + e, z_codes[:], z_scales[:])
-                nc.vector.tensor_tensor(
-                    result[:, 2 * v : 2 * v + 2, :], acc[:].rearrange("p (e j) -> p e j", e=2),
-                    res_sb[:, 2 * v : 2 * v + 2, cols], ALU.add,
-                )
+            return z_codes, z_scales
+
+        def last_layer(b, z_codes, z_scales):
+            cols = slice(P * b, P * (b + 1))
+            acc = bank("o%d" % b, 4 + b)
+            for t in range(4):
+                product(acc[:, P * t : P * (t + 1)], w3d, ws3d, t, z_codes[:], z_scales[:])
+            result = sb("result%d" % b, [P, 4, P], F32)
+            nc.vector.tensor_tensor(result[:], acc[:].rearrange("p (t j) -> p t j", t=4), res_sb[:, :, cols], ALU.add)
             nc.sync.dma_start(out=out_rows[:, :, cols], in_=result[:])
-            rounded = sb("rounded%d" % h, [P, 4 * HALF], BF16)
+            rounded = sb("rounded%d" % b, [P, 512], BF16)
             nc.scalar.copy(
                 out=rounded[:].rearrange("p (c i t) -> p c t i", i=4, t=4),
                 in_=result[:].rearrange("p t (c i) -> p c t i", i=4),
             )
-            return rounded
-
-        def hand_on(h, rounded):
-            cols = slice(HALF * h, HALF * (h + 1))
             quantise(out_codes[:, cols], out_scales[:, cols], rounded[:])
-            nc.sync.dma_start(out=words_of(out_1)[:, cols], in_=out_codes[:, cols].bitcast(I32))
 
-        factors0 = conductance(0)
-        diffs0 = difference(0)
-        factors1 = conductance(1)
-        z0 = flux(0, factors0, diffs0)
-        w3d = deal_aside("w3d", w3, I32)
-        ws3d = deal_aside("ws3d", ws3, U8)
-        diffs1 = difference(1)
-        rounded0 = last_layer(0, z0, w3d, ws3d)
-        z1 = flux(1, factors1, diffs1)
-        rounded1 = last_layer(1, z1, w3d, ws3d)
-        hand_on(0, rounded0)
-        hand_on(1, rounded1)
+        factors = conductance(0) + conductance(1)
+        diffs = difference(0) + difference(1)
+        w3d = deal("w3d", w3, I32)
+        ws3d = deal("ws3d", ws3, U8)
+        fluxes = [flux(b, factors[b], diffs[b]) for b in range(4)]
+        for b in range(4):
+            last_layer(b, *fluxes[b])
+            if b % 2:
+                cols = slice(P * (b - 1), P * (b + 1))
+                nc.sync.dma_start(out=words_of(out_1)[:, cols], in_=out_codes[:, cols].bitcast(I32))
         for q in range(4):
             queue = nc.sync if q % 2 else nc.scalar
             queue.dma_start(

@@ -43,10 +43,10 @@ def tile_picked_harmflux_none_po_kernel(
         def bank(name, number):
             return psum.tile([P, 512], F32, name=name, tag="bank%d" % number)
 
-        def load_scale_rows(plane, scales):
+        def load_scale_rows(plane, first, scales):
             for q in range(4):
                 nc.sync.dma_start(
-                    out=plane[32 * q : 32 * q + 4, :].bitcast(I32),
+                    out=plane[32 * q + first : 32 * q + first + 4, :].bitcast(I32),
                     in_=scales[0, 4 * q : 4 * q + 4, :].bitcast(I32),
                 )
 
@@ -54,56 +54,45 @@ def tile_picked_harmflux_none_po_kernel(
         offs_sb = lists.tile([P, S // 16], U16, name="offs_sb")
         nb_sb = lists.tile([P, S // 16], U16, name="nb_sb")
 
-        zeros = staged("zeros", [P, 27648 // 4], F32, 0)
-        ident = sb("ident", [P, P], F32)
         xs = sb("xs", [P, T], U8)
+        blank = staged("blank", [P, 18944 // 4], I32, 0)
+        ws13 = sb("ws13", [P, 512], U8)
 
         nc.gpsimd.memset(xs[:].bitcast(I32), 0)
-        nc.gpsimd.memset(zeros[:, :P], 0.0)
-        nc.gpsimd.affine_select(
-            out=ident[:], in_=zeros[:, :P], compare_op=ALU.not_equal, fill=1.0, base=0, pattern=[[-1, P]], channel_multiplier=1
-        )
+        nc.gpsimd.memset(blank[:, :P], 0)
+        nc.vector.tensor_copy(ws13[:].bitcast(I32), blank[:, :P])
         nc.sync.dma_start(two_sb[:], two)
         nc.sync.dma_start(offs_sb[:], offs)
         nc.sync.dma_start(nb_sb[:], nb)
-        load_scale_rows(xs, x_scales)
+        load_scale_rows(xs, 0, x_scales)
 
+        gain = staged("gain", [P, 4], F32, 0)
         w2 = staged("w2", [P, 512], I32, 2048)
         ws2 = staged("ws2", [P, 512], U8, 4096)
         xw = staged("xw", [P, T], I32, 6144)
         w1 = staged("w1", [P, 512], I32, 14336)
-        ws1 = staged("ws1", [P, 512], U8, 16384)
-        w3 = staged("w3", [P, 512], I32, 24576)
-        ws3 = staged("ws3", [P, 512], U8, 26624)
-        gain_rows = staged("gain_rows", [P, P], F32, 27136)
-        gain = staged("gain", [P, 4], F32, 0)
+        w3 = staged("w3", [P, 512], I32, 16384)
         nc.gpsimd.memset(ws2[:].bitcast(I32), 0)
-        nc.gpsimd.memset(gain_rows[:], 0.0)
-        nc.gpsimd.memset(ws1[:].bitcast(I32), 0)
-        nc.gpsimd.memset(ws3[:].bitcast(I32), 0)
         nc.sync.dma_start(out=xw[:], in_=words_of(x_words))
         nc.sync.dma_start(out=w2[:], in_=words_of(w2_words))
-        load_scale_rows(ws2, w2_scales)
+        load_scale_rows(ws2, 0, w2_scales)
         nc.sync.dma_start(out=w1[:], in_=words_of(w1_words))
-        nc.sync.dma_start(
-            out=gain_rows[0:4, :].rearrange("t (g i) -> t g i", g=8), in_=gn.rearrange("(g t i) o -> t g (i o)", g=8, t=4)
-        )
-        load_scale_rows(ws1, w1_scales)
+        load_scale_rows(ws13, 0, w1_scales)
+        load_scale_rows(ws13, 4, w3_scales)
+        nc.sync.dma_start(out=gain[:], in_=gn.rearrange("(p t) o -> p (t o)", t=4))
         nc.sync.dma_start(out=w3[:], in_=words_of(w3_words))
-        load_scale_rows(ws3, w3_scales)
 
-        def deal(name, src, dtype):
-            dealt = sb(name, [P, 512], dtype)
+        def deal_words(name, src):
+            dealt = sb(name, [P, 512], I32)
             nc.vector.tensor_copy(
                 out=dealt[:].rearrange("p (t m) -> p m t", t=4), in_=src[:].rearrange("p (m t) -> p m t", t=4)
             )
             return dealt
 
-        def deal_runs(name, src, dtype):
-            dealt = sb(name, [P, 512], dtype)
+        def deal_scales(name, src):
+            dealt = sb(name, [P, 512], U8)
             nc.vector.tensor_copy(
-                out=dealt[:].bitcast(I32).rearrange("p (t g i) -> p t g i", t=4, g=8),
-                in_=src[:].bitcast(I32).rearrange("p (g t i) -> p t g i", t=4, g=8),
+                out=dealt[:].rearrange("p (t m) -> p t m", t=4), in_=src[:].rearrange("p (m t) -> p t m", t=4)
             )
             return dealt
 
@@ -116,105 +105,88 @@ def tile_picked_harmflux_none_po_kernel(
             nc.vector.tensor_copy(picked[:], xw[:].bitcast(U32).indirect(picks[:]))
             return picked
 
-        def product(out, weights, plane, t, codes, scales):
+        def product(out, weights, plane, first, t, codes, scales):
             cols = slice(P * t, P * (t + 1))
             nc.tensor.matmul_mx(
-                out=out, lhsT=weights[:, cols].bitcast(FP8X4), lhsT_scale=plane[:, cols],
+                out=out, lhsT=weights[:, cols].bitcast(FP8X4), lhsT_scale=plane[first:P, cols],
                 rhs=codes.bitcast(FP8X4), rhs_scale=scales, start=True, stop=True,
             )
 
         two_scales = pick_scales("two_scales", two_sb)
         offs_scales = pick_scales("offs_scales", offs_sb)
         two_words = pick_words(sb("two_words", [P, S], U32), two_sb)
-        w2d = deal_runs("w2d", w2, I32)
-        ws2d = deal_runs("ws2d", ws2, U8)
+        w2d = deal_words("w2d", w2)
+        ws2d = deal_scales("ws2d", ws2)
         expo = []
+        expo_own = []
         for t in range(4):
             acc = bank("a%d" % t, t)
-            product(acc[:], w2d, ws2d, t, two_words[:], two_scales[:])
-            e_t = sb("expo%d" % t, [P, S], F32)
-            nc.scalar.activation(out=e_t[:], in_=acc[:], func=ACT.Exp, scale=-1.0)
-            expo.append(e_t)
+            product(acc[:], w2d, ws2d, 0, t, two_words[:], two_scales[:])
+            for name, kept in (("expo", expo), ("expo_own", expo_own)):
+                e_t = sb("%s%d" % (name, t), [P, S], F32)
+                nc.scalar.activation(out=e_t[:], in_=acc[:], func=ACT.Exp, scale=-1.0)
+                kept.append(e_t)
 
         offs_words = pick_words(staged("offs_words", [P, S], U32, 4032), offs_sb)
-        w1d = deal_runs("w1d", w1, I32)
-        ws1d = deal_runs("ws1d", ws1, U8)
-        gain_turned = bank("gain_turned", 7)
-        nc.tensor.transpose(gain_turned[:, :P], gain_rows[:], ident[:])
-        nc.scalar.activation(out=gain[:], in_=gain_turned[:, 0:4], func=ACT.Copy, scale=-2.0)
+        w1d = deal_words("w1d", w1)
+        ws13d = deal_scales("ws13d", ws13)
         res_sb = staged("res_sb", [P, 4, S], F32, 6144)
         nc.sync.dma_start(out=res_sb[:], in_=res.rearrange("(p t) j -> p t j", t=4))
-        vals = []
-        for t in range(4):
+        vals = [sb("vals%d" % t, [P, S], F32) for t in range(4)]
+        vals_own = [sb("vals_own%d" % t, [P, S], F32) for t in range(4)]
+        for t in (1, 0, 2, 3):
             acc = bank("y%d" % t, 4 + t)
-            product(acc[:], w1d, ws1d, t, offs_words[:], offs_scales[:])
-            y_t = sb("vals%d" % t, [P, S], F32)
-            nc.scalar.activation(out=y_t[:], in_=acc[:], func=ACT.Copy, scale=gain[:, t : t + 1])
-            vals.append(y_t)
+            product(acc[:], w1d, ws13d, 0, t, offs_words[:], offs_scales[:])
+            nc.scalar.activation(out=vals[t][:], in_=acc[:], func=ACT.Copy, scale=gain[:, t : t + 1])
+            if t == 0:
+                nc.scalar.activation(out=vals_own[t][:], in_=acc[:], func=ACT.Copy, scale=gain[:, t : t + 1])
+            else:
+                nc.sync.dma_start(out=vals_own[t][:], in_=vals[t][:])
 
-        def turned_sum(name, number, b, own, fetched):
-            acc = bank(name, number)
-            steps = [(own[t][:, P * b : P * (b + 1)], t) for t in range(4)]
-            steps = steps + [(fetched[t][:, P * (b % 2) : P * (b % 2 + 1)], t) for t in range(4)]
-            for n, (src, t) in enumerate(steps):
-                nc.tensor.matmul(
-                    acc[:, P * t : P * (t + 1)], lhsT=src, rhs=ident[:],
-                    start=(n == 0), stop=(n == len(steps) - 1), is_transpose=True,
-                )
-            return acc
-
-        def paired(ap):
-            return ap.rearrange("j (t g i) -> j g t i", t=4, g=8)
-
-        def woven(ap):
-            return ap.rearrange("j (g t i) -> j g t i", t=4, g=8)
-
-        def nb_slice(h):
-            return nb_sb[:, 16 * h : 16 * (h + 1)]
-
-        expo_near = staged("expo_near", [P, 4 * S], F32, 16320)
-
-        def conductance(h):
-            fetched = []
+        def meet_neighbours(name, window, own, op):
+            met = sb(name, [P, 4 * S], F32)
             for t in range(4):
-                g = expo_near[:, S * t + HALF * h : S * t + HALF * (h + 1)]
-                nc.vector.tensor_copy(g, expo[t][:].indirect(nb_slice(h)))
-                fetched.append(g)
-            factors = []
-            for b in (2 * h, 2 * h + 1):
-                acc = turned_sum("s%d" % b, b, b, expo, fetched)
-                root = staged("root0", [P, 512], F32, 0) if b == 0 else sb("root%d" % b, [P, 512], F32)
-                nc.scalar.activation(out=woven(root[:]), in_=paired(acc[:]), func=ACT.Abs_reciprocal_sqrt, scale=0.5, bias=1.0)
-                factor = sb("factor%d" % b, [P, 512], F32)
-                nc.scalar.activation(out=factor[:], in_=root[:], func=ACT.Square)
-                factors.append(factor)
-            return factors
+                for h in range(2):
+                    nc.vector.tensor_tensor(
+                        met[:, S * t + HALF * h : S * t + HALF * (h + 1)],
+                        window[t][:].indirect(nb_sb[:, 16 * h : 16 * (h + 1)]),
+                        own[t][:, HALF * h : HALF * (h + 1)], op,
+                    )
+            return met[:].rearrange("p (t j) -> p t j", t=4)
 
-        def difference(h):
-            fetched = []
-            for t in range(4):
-                g = sb("yn%d_%d" % (h, t), [P, HALF], F32)
-                nc.vector.tensor_scalar(g[:], vals[t][:].indirect(nb_slice(h)), -1.0, 0.0, ALU.mult, ALU.add)
-                fetched.append(g)
-            return [turned_sum("d%d" % b, 4 + b, b, vals, fetched) for b in (2 * h, 2 * h + 1)]
+        sums = meet_neighbours("sums", expo, expo_own, ALU.add)
+        w3d = deal_words("w3d", w3)
+        diffs = meet_neighbours("diffs", vals, vals_own, ALU.subtract)
+
+        factors = []
+        for b in range(4):
+            root = staged("root0", [P, 512], F32, 0) if b == 0 else sb("root%d" % b, [P, 512], F32)
+            nc.scalar.activation(
+                out=root[:].rearrange("p (t j) -> p t j", t=4), in_=sums[:, :, P * b : P * (b + 1)],
+                func=ACT.Abs_reciprocal_sqrt, scale=0.25, bias=0.5,
+            )
+            factor = sb("factor%d" % b, [P, 512], F32)
+            nc.scalar.activation(out=factor[:], in_=root[:], func=ACT.Square)
+            factors.append(factor)
 
         def quantise(codes, scales, values):
             nc.vector.quantize_mx(out=codes.bitcast(FP8X4), scales=scales, in_=values)
+
+        def by_fours(ap):
+            return ap.rearrange("p t (c i) -> p c t i", i=4)
+
+        def woven(ap):
+            return ap.rearrange("p (c i t) -> p c t i", i=4, t=4)
 
         out_rows = out_0.rearrange("(p t) j -> p t j", t=4)
         out_codes = sb("out_codes", [P, S], U32)
         out_scales = sb("out_scales", [P, S], U8)
 
-        def flux(b, factor, diff):
-            zt = sb("zt%d" % b, [P, 512], BF16)
-            nc.vector.tensor_tensor(woven(zt[:]), paired(diff[:]), woven(factor[:]), ALU.mult)
-            back = bank("z%d" % b, b)
-            for u in range(2):
-                nc.tensor.transpose(back[:, P * u : P * (u + 1)], zt[:].bitcast(F32)[:, u : 2 * P : 2], ident[:])
+        def flux(b):
             z = sb("z%d" % b, [P, 512], BF16)
-            nc.scalar.copy(
-                out=z[:].bitcast(F32).rearrange("p (j u) -> p j u", u=2),
-                in_=back[:, : 2 * P].rearrange("p (u j) -> p j u", u=2),
+            nc.vector.tensor_tensor(
+                woven(z[:]), by_fours(diffs[:, :, P * b : P * (b + 1)]),
+                by_fours(factors[b][:].rearrange("p (t j) -> p t j", t=4)), ALU.mult,
             )
             z_codes = sb("z_codes%d" % b, [P, P], U32)
             z_scales = sb("z_scales%d" % b, [P, P], U8)
@@ -223,24 +195,17 @@ def tile_picked_harmflux_none_po_kernel(
 
         def last_layer(b, z_codes, z_scales):
             cols = slice(P * b, P * (b + 1))
-            acc = bank("o%d" % b, 4 + b)
+            acc = bank("o%d" % b, b)
             for t in range(4):
-                product(acc[:, P * t : P * (t + 1)], w3d, ws3d, t, z_codes[:], z_scales[:])
+                product(acc[:, P * t : P * (t + 1)], w3d, ws13d, 4, t, z_codes[:], z_scales[:])
             result = sb("result%d" % b, [P, 4, P], F32)
             nc.vector.tensor_tensor(result[:], acc[:].rearrange("p (t j) -> p t j", t=4), res_sb[:, :, cols], ALU.add)
             nc.sync.dma_start(out=out_rows[:, :, cols], in_=result[:])
             rounded = sb("rounded%d" % b, [P, 512], BF16)
-            nc.scalar.copy(
-                out=rounded[:].rearrange("p (c i t) -> p c t i", i=4, t=4),
-                in_=result[:].rearrange("p t (c i) -> p c t i", i=4),
-            )
+            nc.scalar.copy(out=woven(rounded[:]), in_=by_fours(result[:]))
             quantise(out_codes[:, cols], out_scales[:, cols], rounded[:])
 
-        factors = conductance(0) + conductance(1)
-        diffs = difference(0) + difference(1)
-        w3d = deal("w3d", w3, I32)
-        ws3d = deal("ws3d", ws3, U8)
-        fluxes = [flux(b, factors[b], diffs[b]) for b in range(4)]
+        fluxes = [flux(b) for b in range(4)]
         for b in range(4):
             last_layer(b, *fluxes[b])
             if b % 2:

from contextlib import ExitStack

import concourse.mybir as mybir

F32 = mybir.dt.float32
BF16 = mybir.dt.bfloat16
I32 = mybir.dt.int32
U32 = mybir.dt.uint32
U16 = mybir.dt.uint16
U8 = mybir.dt.uint8
FP8X4 = mybir.dt.float8_e4m3fn_x4
ACT = mybir.ActivationFunctionType
ALU = mybir.AluOpType

P = 128
T = 2048
S = 512
HALF = 256
FLOPS = 3 * 2 * 512 * 512 * 512


def words_of(packed):
    return packed[0].rearrange("p n t -> p (n t)").bitcast(I32)


def tile_picked_harmflux_none_po_kernel(
    tc, x_words, x_scales, w1_words, w1_scales, w2_words, w2_scales, gn, w3_words, w3_scales, res, offs, two, nb,
    out_0, out_1, out_2,
):
    nc = tc.nc
    with ExitStack() as ctx:
        lists = ctx.enter_context(tc.tile_pool(name="lists", bufs=1))
        keep = ctx.enter_context(tc.tile_pool(name="keep", bufs=1))
        stage = ctx.enter_context(tc.tile_pool(name="stage", bufs=1))
        psum = ctx.enter_context(tc.psum_pool(name="psum", bufs=1))

        def sb(name, shape, dtype):
            return keep.tile(shape, dtype, name=name, align_bytes=64)

        def staged(name, shape, dtype, offset):
            return stage.tile(shape, dtype, name=name, offset=offset, align_bytes=64)

        def bank(name, number):
            return psum.tile([P, 512], F32, name=name, tag="bank%d" % number)

        def load_scale_rows(plane, first, scales):
            for q in range(4):
                nc.sync.dma_start(
                    out=plane[32 * q + first : 32 * q + first + 4, :].bitcast(I32),
                    in_=scales[0, 4 * q : 4 * q + 4, :].bitcast(I32),
                )

        two_sb = lists.tile([P, S // 16], U16, name="two_sb")
        offs_sb = lists.tile([P, S // 16], U16, name="offs_sb")
        nb_sb = lists.tile([P, S // 16], U16, name="nb_sb")

        xs = sb("xs", [P, T], U8)
        blank = staged("blank", [P, 18944 // 4], I32, 0)
        ws13 = sb("ws13", [P, 512], U8)

        nc.gpsimd.memset(xs[:].bitcast(I32), 0)
        nc.gpsimd.memset(blank[:, :P], 0)
        nc.vector.tensor_copy(ws13[:].bitcast(I32), blank[:, :P])
        nc.sync.dma_start(two_sb[:], two)
        nc.sync.dma_start(offs_sb[:], offs)
        nc.sync.dma_start(nb_sb[:], nb)
        load_scale_rows(xs, 0, x_scales)

        gain = staged("gain", [P, 4], F32, 0)
        w2 = staged("w2", [P, 512], I32, 2048)
        ws2 = staged("ws2", [P, 512], U8, 4096)
        xw = staged("xw", [P, T], I32, 6144)
        w1 = staged("w1", [P, 512], I32, 14336)
        w3 = staged("w3", [P, 512], I32, 16384)
        nc.gpsimd.memset(ws2[:].bitcast(I32), 0)
        nc.sync.dma_start(out=xw[:], in_=words_of(x_words))
        nc.sync.dma_start(out=w2[:], in_=words_of(w2_words))
        load_scale_rows(ws2, 0, w2_scales)
        nc.sync.dma_start(out=w1[:], in_=words_of(w1_words))
        load_scale_rows(ws13, 0, w1_scales)
        load_scale_rows(ws13, 4, w3_scales)
        nc.sync.dma_start(out=gain[:], in_=gn.rearrange("(p t) o -> p (t o)", t=4))
        nc.sync.dma_start(out=w3[:], in_=words_of(w3_words))

        def deal_words(name, src):
            dealt = sb(name, [P, 512], I32)
            nc.vector.tensor_copy(
                out=dealt[:].rearrange("p (t m) -> p m t", t=4), in_=src[:].rearrange("p (m t) -> p m t", t=4)
            )
            return dealt

        def deal_scales(name, src):
            dealt = sb(name, [P, 512], U8)
            nc.vector.tensor_copy(
                out=dealt[:].rearrange("p (t m) -> p t m", t=4), in_=src[:].rearrange("p (m t) -> p t m", t=4)
            )
            return dealt

        def pick_scales(name, picks):
            picked = sb(name, [P, S], U8)
            nc.vector.tensor_copy(picked[:], xs[:].indirect(picks[:]))
            return picked

        def pick_words(picked, picks):
            nc.vector.tensor_copy(picked[:], xw[:].bitcast(U32).indirect(picks[:]))
            return picked

        def product(out, weights, plane, first, t, codes, scales):
            cols = slice(P * t, P * (t + 1))
            nc.tensor.matmul_mx(
                out=out, lhsT=weights[:, cols].bitcast(FP8X4), lhsT_scale=plane[first:P, cols],
                rhs=codes.bitcast(FP8X4), rhs_scale=scales, start=True, stop=True,
            )

        two_scales = pick_scales("two_scales", two_sb)
        offs_scales = pick_scales("offs_scales", offs_sb)
        two_words = pick_words(sb("two_words", [P, S], U32), two_sb)
        w2d = deal_words("w2d", w2)
        ws2d = deal_scales("ws2d", ws2)
        expo = []
        expo_own = []
        for t in range(4):
            acc = bank("a%d" % t, t)
            product(acc[:], w2d, ws2d, 0, t, two_words[:], two_scales[:])
            for name, kept in (("expo", expo), ("expo_own", expo_own)):
                e_t = sb("%s%d" % (name, t), [P, S], F32)
                nc.scalar.activation(out=e_t[:], in_=acc[:], func=ACT.Exp, scale=-1.0)
                kept.append(e_t)

        offs_words = pick_words(staged("offs_words", [P, S], U32, 4032), offs_sb)
        w1d = deal_words("w1d", w1)
        ws13d = deal_scales("ws13d", ws13)
        res_sb = staged("res_sb", [P, 4, S], F32, 6144)
        nc.sync.dma_start(out=res_sb[:], in_=res.rearrange("(p t) j -> p t j", t=4))
        vals = [sb("vals%d" % t, [P, S], F32) for t in range(4)]
        vals_own = [sb("vals_own%d" % t, [P, S], F32) for t in range(4)]
        for t in (1, 0, 2, 3):
            acc = bank("y%d" % t, 4 + t)
            product(acc[:], w1d, ws13d, 0, t, offs_words[:], offs_scales[:])
            nc.scalar.activation(out=vals[t][:], in_=acc[:], func=ACT.Copy, scale=gain[:, t : t + 1])
            if t == 0:
                nc.scalar.activation(out=vals_own[t][:], in_=acc[:], func=ACT.Copy, scale=gain[:, t : t + 1])
            else:
                nc.sync.dma_start(out=vals_own[t][:], in_=vals[t][:])

        def meet_neighbours(name, window, own, op):
            met = sb(name, [P, 4 * S], F32)
            for t in range(4):
                for h in range(2):
                    nc.vector.tensor_tensor(
                        met[:, S * t + HALF * h : S * t + HALF * (h + 1)],
                        window[t][:].indirect(nb_sb[:, 16 * h : 16 * (h + 1)]),
                        own[t][:, HALF * h : HALF * (h + 1)], op,
                    )
            return met[:].rearrange("p (t j) -> p t j", t=4)

        sums = meet_neighbours("sums", expo, expo_own, ALU.add)
        w3d = deal_words("w3d", w3)
        diffs = meet_neighbours("diffs", vals, vals_own, ALU.subtract)

        factors = []
        for b in range(4):
            root = staged("root0", [P, 512], F32, 0) if b == 0 else sb("root%d" % b, [P, 512], F32)
            nc.scalar.activation(
                out=root[:].rearrange("p (t j) -> p t j", t=4), in_=sums[:, :, P * b : P * (b + 1)],
                func=ACT.Abs_reciprocal_sqrt, scale=0.25, bias=0.5,
            )
            factor = sb("factor%d" % b, [P, 512], F32)
            nc.scalar.activation(out=factor[:], in_=root[:], func=ACT.Square)
            factors.append(factor)

        def quantise(codes, scales, values):
            nc.vector.quantize_mx(out=codes.bitcast(FP8X4), scales=scales, in_=values)

        def by_fours(ap):
            return ap.rearrange("p t (c i) -> p c t i", i=4)

        def woven(ap):
            return ap.rearrange("p (c i t) -> p c t i", i=4, t=4)

        out_rows = out_0.rearrange("(p t) j -> p t j", t=4)
        out_codes = sb("out_codes", [P, S], U32)
        out_scales = sb("out_scales", [P, S], U8)

        def flux(b):
            z = sb("z%d" % b, [P, 512], BF16)
            nc.vector.tensor_tensor(
                woven(z[:]), by_fours(diffs[:, :, P * b : P * (b + 1)]),
                by_fours(factors[b][:].rearrange("p (t j) -> p t j", t=4)), ALU.mult,
            )
            z_codes = sb("z_codes%d" % b, [P, P], U32)
            z_scales = sb("z_scales%d" % b, [P, P], U8)
            quantise(z_codes[:], z_scales[:], z[:])
            return z_codes, z_scales

        def last_layer(b, z_codes, z_scales):
            cols = slice(P * b, P * (b + 1))
            acc = bank("o%d" % b, b)
            for t in range(4):
                product(acc[:, P * t : P * (t + 1)], w3d, ws13d, 4, t, z_codes[:], z_scales[:])
            result = sb("result%d" % b, [P, 4, P], F32)
            nc.vector.tensor_tensor(result[:], acc[:].rearrange("p (t j) -> p t j", t=4), res_sb[:, :, cols], ALU.add)
            nc.sync.dma_start(out=out_rows[:, :, cols], in_=result[:])
            rounded = sb("rounded%d" % b, [P, 512], BF16)
            nc.scalar.copy(out=woven(rounded[:]), in_=by_fours(result[:]))
            quantise(out_codes[:, cols], out_scales[:, cols], rounded[:])

        fluxes = [flux(b) for b in range(4)]
        for b in range(4):
            last_layer(b, *fluxes[b])
            if b % 2:
                cols = slice(P * (b - 1), P * (b + 1))
                nc.sync.dma_start(out=words_of(out_1)[:, cols], in_=out_codes[:, cols].bitcast(I32))
        for q in range(4):
            queue = nc.sync if q % 2 else nc.scalar
            queue.dma_start(
                out=out_2[0, 4 * q : 4 * q + 4, :].bitcast(I32), in_=out_scales[32 * q : 32 * q + 4, :].bitcast(I32)
            )
